import numpy as np
import ml_dtypes


def mxq(x, axis, fmt="e4m3"):
    dtype, down = {"e4m3": (ml_dtypes.float8_e4m3fn, 7), "e5m2": (ml_dtypes.float8_e5m2, 14)}[fmt]
    v = np.moveaxis(np.asarray(x, np.float32).astype(ml_dtypes.bfloat16).astype(np.float64), axis, -1)
    blocks = v.reshape(v.shape[:-1] + (-1, 32))
    amax = np.abs(blocks).max(-1, keepdims=True)
    byte = np.maximum(np.where(amax > 0, np.frexp(amax)[1] - 1 + 127, 0) - down, 1)
    scale = np.exp2(byte - 127.0)
    codes = (blocks / scale).astype(np.float32).astype(dtype).astype(np.float64)
    return np.moveaxis((codes * scale).reshape(v.shape), -1, axis)


WIDE = False


def mx_kscale(k):
    if not WIDE:
        return np.ones(k)
    levels = np.array([10, -10, 5, -5, 0])
    if k % 512:
        return np.exp2(np.random.permutation(np.resize(levels, k // 32))).repeat(32)
    a = np.empty((k // 512, 16))
    for p in range(k // 512):
        a[p, :8] = np.random.permutation(np.resize(levels, 8))
        for g in range(8):
            far = levels[np.abs(levels - a[p, g]) >= 10]
            a[p, g + 8] = far[np.random.randint(len(far))]
    return np.exp2(a.ravel()).repeat(32)


def f64(x):
    return np.asarray(x).astype(np.float64)


def striped(idx):
    return np.tile(idx.reshape(-1, 16).T, (8, 1)).astype(np.uint16)


def unstriped(offs):
    return offs[:16].T.reshape(-1).astype(np.int64)


E2M1 = np.array([0.0, 0.5, 1.0, 1.5, 2.0, 3.0, 4.0, 6.0, -0.0, -0.5, -1.0, -1.5, -2.0, -3.0, -4.0, -6.0])


def pack_fp4(w):
    k, n = w.shape
    w = f64(np.asarray(w, np.float32).astype(ml_dtypes.bfloat16)).reshape(k // 32, 32, n)
    amax = np.abs(w).max(1)
    mant, ex = np.frexp(amax / 6.0)
    byte = np.clip(np.where(amax > 0, np.where(mant > 0.5, ex, ex - 1) + 127, 1), 1, 254)
    scaled = (w * np.exp2(127.0 - byte)[:, None, :]).reshape(k, n).astype(np.float32)
    c = np.ascontiguousarray(scaled.reshape(k // 512, 128, 4, n).transpose(0, 1, 3, 2)).astype(ml_dtypes.float4_e2m1fn).view(np.uint8) & 0xF
    words = (c[..., 0::2] | (c[..., 1::2] << 4)).reshape(k // 512, 128, 2 * n)
    return np.ascontiguousarray(words), np.ascontiguousarray(byte.astype(np.uint8).reshape(k // 512, 16, n))


def unpack_fp4(words, scales):
    g, _, n = scales.shape
    words = np.ascontiguousarray(words).reshape(g, 128, n, 2)
    nib = np.empty((g, 128, n, 4), np.uint8)
    nib[..., 0::2] = words & 0xF
    nib[..., 1::2] = words >> 4
    vals = E2M1[nib] * np.repeat(np.exp2(scales.astype(np.float64) - 127.0), 8, axis=1)[..., None]
    return vals.transpose(0, 1, 3, 2).reshape(g * 512, n)


K, T, S, N = 1024, 1024, 512, 128


def setup_inputs():
    n = np.random.standard_normal
    s = mx_kscale(K)[:, None]
    packed_w1 = pack_fp4(n((K, N)) / np.sqrt(2 * K) / s)
    packed_w2 = pack_fp4(n((K, N)) / np.sqrt(2 * K) / s)
    return {
        "xT": (n((K, T)) * s).astype(np.float32),
        "w1_words": packed_w1[0],
        "w1_scales": packed_w1[1],
        "w2_words": packed_w2[0],
        "w2_scales": packed_w2[1],
        "offs": striped(np.random.permutation(T)[:S]),
    }


def reference(xT, w1_words, w1_scales, w2_words, w2_scales, offs):
    xq = mxq(f64(xT)[:, unstriped(offs)], 0, "e4m3")
    y0 = unpack_fp4(w1_words, w1_scales).T @ xq
    y1 = unpack_fp4(w2_words, w2_scales).T @ xq
    return y0 + np.pad(y1, ((0, 0), (1, 0)))[:, :S]

@@ -1,0 +1,140 @@
+from contextlib import ExitStack
+
+import concourse.mybir as mybir
+
+K, T, S, M = 1024, 1024, 512, 128
+FLOPS = 2 * 2 * K * M * S
+
+F32 = mybir.dt.float32
+BF16 = mybir.dt.bfloat16
+I32 = mybir.dt.int32
+U32 = mybir.dt.uint32
+U16 = mybir.dt.uint16
+U8 = mybir.dt.uint8
+FP8X4 = mybir.dt.float8_e4m3fn_x4
+FP4X4 = mybir.dt.float4_e2m1fn_x4
+
+P = 128
+PASSES = 2
+CHUNK = 128
+CHUNKS = S // CHUNK
+LIST_COLS = CHUNK // 16
+
+
+def tile_picked_listconv_none_e_kernel(tc, xT, w1_words, w1_scales, w2_words, w2_scales, offs, out):
+    nc = tc.nc
+    x_rows = xT.rearrange("(z p j) t -> z p j t", z=PASSES, j=4)
+
+    with ExitStack() as ctx:
+        keep = ctx.enter_context(tc.tile_pool(name="keep", bufs=1))
+        psum = ctx.enter_context(tc.psum_pool(name="psum", bufs=1))
+
+        offsets = keep.tile([P, S // 16], U16, name="offsets")
+        nc.sync.dma_start(offsets[:], offs)
+
+        pieces = {}
+        for z in range(PASSES):
+            for u in range(2):
+                spans = [(0, T // 2), (T // 2, T)] if (z, u) == (PASSES - 1, 1) else [(0, T)]
+                pieces[z, u] = []
+                for a, b in spans:
+                    raw = keep.tile([P, 2, b - a], F32, name=f"raw{z}{u}_{a}")
+                    nc.sync.dma_start(raw[:], x_rows[z][:, 2 * u : 2 * u + 2, a:b])
+                    pieces[z, u].append((a, b, raw))
+
+        w_codes = []
+        w_scales = []
+        for d, words in enumerate((w1_words, w2_words)):
+            codes = keep.tile([P, PASSES, 2 * M], U8, name=f"w_codes{d}", align_bytes=64)
+            nc.sync.dma_start(codes[:].bitcast(I32), words.rearrange("z p c -> p z c").bitcast(I32))
+            w_codes.append(codes)
+        for d, (scales, queue) in enumerate(((w1_scales, nc.sync), (w2_scales, nc.gpsimd))):
+            plane = keep.tile([P, PASSES, M], U8, name=f"w_scales{d}", align_bytes=64)
+            nc.gpsimd.memset(plane[:].bitcast(I32), 0)
+            rows = scales.rearrange("z (q r) c -> r q z c", r=4)
+            for r in range(4):
+                queue.dma_start(plane[r:P:32, :, :].bitcast(I32), rows[r].bitcast(I32))
+            w_scales.append(plane)
+
+        tap1 = keep.tile([P, S], F32, name="tap1")
+        nc.vector.memset(tap1[:, 0:1], 0.0)
+
+        def cast(pairs, a, b, raw, scalar_cols):
+            mid = b - scalar_cols
+            if mid > a:
+                nc.vector.tensor_copy(pairs[:, a:mid, :], raw[:, :, 0 : mid - a].rearrange("p e t -> p t e"))
+            nc.scalar.copy(pairs[:, mid:b, :], raw[:, :, mid - a : b - a].rearrange("p e t -> p t e"))
+
+        def window(pairs):
+            return pairs[:].rearrange("p t e -> p (t e)").bitcast(U32)
+
+        def words_of(picked):
+            return picked[:].rearrange("p n j -> p (n j)").bitcast(U32).rearrange("p (n u) -> p n u", u=2)
+
+        pair_tiles = {}
+        for z in range(PASSES):
+            for u in range(2):
+                pair_tiles[z, u] = keep.tile([P, T, 2], BF16, name=f"pairs{z}{u}")
+
+        banks = {(d, c): psum.tile([M, CHUNK], F32, name=f"bank{d}{c}") for c in range(CHUNKS) for d in range(2)}
+
+        def multiply(z, c, codes, scales):
+            for d in (1, 0):
+                nc.tensor.matmul_mx(
+                    out=banks[d, c][:],
+                    lhsT=w_codes[d][:, z, :].bitcast(FP4X4),
+                    lhsT_scale=w_scales[d][:, z, :],
+                    rhs=codes.bitcast(FP8X4),
+                    rhs_scale=scales,
+                    start=(z == 0),
+                    stop=(z == PASSES - 1),
+                )
+
+        picked0 = keep.tile([P, S, 4], BF16, name="picked0", align_bytes=64)
+        for u in range(2):
+            a, b, raw = pieces[0, u][0]
+            cast(pair_tiles[0, u], a, b, raw, 352)
+            nc.vector.tensor_copy(words_of(picked0)[:, :, u], window(pair_tiles[0, u]).indirect(offsets[:]))
+        codes0 = keep.tile([P, S], U32, name="codes0", align_bytes=64)
+        scales0 = keep.tile([P, S], U8, name="scales0", align_bytes=64)
+        nc.vector.quantize_mx(out=codes0[:].bitcast(FP8X4), scales=scales0[:], in_=picked0[:].rearrange("p n j -> p (n j)"))
+        for c in range(CHUNKS):
+            cols = slice(c * CHUNK, (c + 1) * CHUNK)
+            multiply(0, c, codes0[:, cols], scales0[:, cols])
+
+        picked1 = [keep.tile([P, CHUNK, 4], BF16, name=f"picked1_{c}", align_bytes=64) for c in range(CHUNKS)]
+
+        def gather1(u, c):
+            entries = offsets[:, c * LIST_COLS : (c + 1) * LIST_COLS]
+            nc.vector.tensor_copy(words_of(picked1[c])[:, :, u], window(pair_tiles[1, u]).indirect(entries))
+
+        a, b, raw = pieces[1, 0][0]
+        cast(pair_tiles[1, 0], a, b, raw, 352)
+        for c in range(CHUNKS):
+            gather1(0, c)
+        a, b, raw = pieces[1, 1][0]
+        cast(pair_tiles[1, 1], a, b, raw, b - a)
+        a, b, raw = pieces[1, 1][1]
+        cast(pair_tiles[1, 1], a, b, raw, 160)
+
+        def quantize1(c):
+            codes = keep.tile([P, CHUNK], U32, name=f"codes1_{c}", align_bytes=64)
+            scales = keep.tile([P, CHUNK], U8, name=f"scales1_{c}", align_bytes=64)
+            nc.vector.quantize_mx(out=codes[:].bitcast(FP8X4), scales=scales[:], in_=picked1[c][:].rearrange("p n j -> p (n j)"))
+            multiply(1, c, codes[:], scales[:])
+            width = min(CHUNK, S - 1 - c * CHUNK)
+            nc.scalar.copy(tap1[:, 1 + c * CHUNK : 1 + c * CHUNK + width], banks[1, c][:, 0:width])
+
+        def finish(c):
+            cols = slice(c * CHUNK, (c + 1) * CHUNK)
+            result = keep.tile([M, CHUNK], F32, name=f"result{c}")
+            nc.vector.tensor_tensor(result[:], banks[0, c][:], tap1[:, cols], mybir.AluOpType.add)
+            nc.sync.dma_start(out[:, cols], result[:])
+
+        gather1(1, 0)
+        for c in range(CHUNKS):
+            if c + 1 < CHUNKS:
+                gather1(1, c + 1)
+            quantize1(c)
+        for c in range(CHUNKS):
+            finish(c)

@@ -19,6 +19,8 @@ PASSES = 2
 CHUNK = 128
 CHUNKS = S // CHUNK
 LIST_COLS = CHUNK // 16
+HALF = T // 2
+VECTOR_COLS = 320
 
 
 def tile_picked_listconv_none_e_kernel(tc, xT, w1_words, w1_scales, w2_words, w2_scales, offs, out):
@@ -28,113 +30,99 @@ def tile_picked_listconv_none_e_kernel(tc, xT, w1_words, w1_scales, w2_words, w2
     with ExitStack() as ctx:
         keep = ctx.enter_context(tc.tile_pool(name="keep", bufs=1))
         psum = ctx.enter_context(tc.psum_pool(name="psum", bufs=1))
+        raw = {}
+        w_codes = {}
+        w_scales = {}
 
-        offsets = keep.tile([P, S // 16], U16, name="offsets")
-        nc.sync.dma_start(offsets[:], offs)
+        def load_x(z, u, h):
+            raw[z, u, h] = keep.tile([P, 2, HALF], F32, name=f"raw{z}{u}{h}", tag="staging", bufs=4, align_bytes=64)
+            nc.sync.dma_start(raw[z, u, h][:], x_rows[z][:, 2 * u : 2 * u + 2, h * HALF : (h + 1) * HALF])
 
-        pieces = {}
-        for z in range(PASSES):
-            for u in range(2):
-                spans = [(0, T // 2), (T // 2, T)] if (z, u) == (PASSES - 1, 1) else [(0, T)]
-                pieces[z, u] = []
-                for a, b in spans:
-                    raw = keep.tile([P, 2, b - a], F32, name=f"raw{z}{u}_{a}")
-                    nc.sync.dma_start(raw[:], x_rows[z][:, 2 * u : 2 * u + 2, a:b])
-                    pieces[z, u].append((a, b, raw))
-
-        w_codes = []
-        w_scales = []
-        for d, words in enumerate((w1_words, w2_words)):
-            codes = keep.tile([P, PASSES, 2 * M], U8, name=f"w_codes{d}", align_bytes=64)
-            nc.sync.dma_start(codes[:].bitcast(I32), words.rearrange("z p c -> p z c").bitcast(I32))
-            w_codes.append(codes)
-        for d, (scales, queue) in enumerate(((w1_scales, nc.sync), (w2_scales, nc.gpsimd))):
-            plane = keep.tile([P, PASSES, M], U8, name=f"w_scales{d}", align_bytes=64)
-            nc.gpsimd.memset(plane[:].bitcast(I32), 0)
+        def load_scales(d, scales, tag):
+            w_scales[d] = keep.tile([P, PASSES, M], U8, name=f"w_scales{d}", tag=tag, align_bytes=64)
+            nc.gpsimd.memset(w_scales[d][:].bitcast(I32), 0)
             rows = scales.rearrange("z (q r) c -> r q z c", r=4)
             for r in range(4):
-                queue.dma_start(plane[r:P:32, :, :].bitcast(I32), rows[r].bitcast(I32))
-            w_scales.append(plane)
+                nc.sync.dma_start(w_scales[d][r:P:32, :, :].bitcast(I32), rows[r].bitcast(I32))
+
+        def load_words(d, words):
+            w_codes[d] = keep.tile([P, PASSES, 2 * M], U8, name=f"w_codes{d}", tag="staging", bufs=4, align_bytes=64)
+            nc.sync.dma_start(w_codes[d][:].bitcast(I32), words.rearrange("z p c -> p z c").bitcast(I32))
+
+        halves = [(z, u, h) for z in range(PASSES) for u in range(2) for h in range(2)]
+        load_x(*halves[0])
+        offsets = keep.tile([P, S // 16], U16, name="offsets")
+        nc.sync.dma_start(offsets[:], offs)
+        load_scales(1, w2_scales, "w_scales1")
+        for half in halves[1:]:
+            load_x(*half)
+        load_words(1, w2_words)
+        load_words(0, w1_words)
 
         tap1 = keep.tile([P, S], F32, name="tap1")
-        nc.vector.memset(tap1[:, 0:1], 0.0)
+        nc.gpsimd.memset(tap1[:, 0:1], 0.0)
 
-        def cast(pairs, a, b, raw, scalar_cols):
-            mid = b - scalar_cols
-            if mid > a:
-                nc.vector.tensor_copy(pairs[:, a:mid, :], raw[:, :, 0 : mid - a].rearrange("p e t -> p t e"))
-            nc.scalar.copy(pairs[:, mid:b, :], raw[:, :, mid - a : b - a].rearrange("p e t -> p t e"))
-
-        def window(pairs):
+        def cast(z, u):
+            pairs = keep.tile([P, T, 2], BF16, name=f"pairs{z}{u}", tag=f"pairs{z}{u}", align_bytes=64)
+            for h in range(2):
+                source = raw[z, u, h][:].rearrange("p e t -> p t e")
+                target = pairs[:, h * HALF : (h + 1) * HALF, :]
+                split = VECTOR_COLS if (h == 1 or (z, u) == (0, 0)) else 0
+                if (z, u, h) == (1, 0, 1):
+                    split = 128
+                if split:
+                    nc.vector.tensor_copy(target[:, 0:split, :], source[:, 0:split, :])
+                nc.scalar.copy(target[:, split:HALF, :], source[:, split:HALF, :])
             return pairs[:].rearrange("p t e -> p (t e)").bitcast(U32)
-
-        def words_of(picked):
-            return picked[:].rearrange("p n j -> p (n j)").bitcast(U32).rearrange("p (n u) -> p n u", u=2)
-
-        pair_tiles = {}
-        for z in range(PASSES):
-            for u in range(2):
-                pair_tiles[z, u] = keep.tile([P, T, 2], BF16, name=f"pairs{z}{u}")
 
         banks = {(d, c): psum.tile([M, CHUNK], F32, name=f"bank{d}{c}") for c in range(CHUNKS) for d in range(2)}
 
-        def multiply(z, c, codes, scales):
+        codes = keep.tile([P, S], U32, name="codes", align_bytes=64)
+        scales = keep.tile([P, S], U8, name="scales", align_bytes=64)
+
+        def quantize(cols, words):
+            values = words.rearrange("p n u -> p (n u)").bitcast(BF16)
+            nc.vector.quantize_mx(out=codes[:, cols].bitcast(FP8X4), scales=scales[:, cols], in_=values)
+
+        def multiply(z, c):
+            cols = slice(c * CHUNK, (c + 1) * CHUNK)
             for d in (1, 0):
                 nc.tensor.matmul_mx(
                     out=banks[d, c][:],
                     lhsT=w_codes[d][:, z, :].bitcast(FP4X4),
                     lhsT_scale=w_scales[d][:, z, :],
-                    rhs=codes.bitcast(FP8X4),
-                    rhs_scale=scales,
+                    rhs=codes[:, cols].bitcast(FP8X4),
+                    rhs_scale=scales[:, cols],
                     start=(z == 0),
                     stop=(z == PASSES - 1),
                 )
 
-        picked0 = keep.tile([P, S, 4], BF16, name="picked0", align_bytes=64)
+        picked0 = keep.tile([P, S, 2], U32, name="picked0", align_bytes=64)
         for u in range(2):
-            a, b, raw = pieces[0, u][0]
-            cast(pair_tiles[0, u], a, b, raw, 352)
-            nc.vector.tensor_copy(words_of(picked0)[:, :, u], window(pair_tiles[0, u]).indirect(offsets[:]))
-        codes0 = keep.tile([P, S], U32, name="codes0", align_bytes=64)
-        scales0 = keep.tile([P, S], U8, name="scales0", align_bytes=64)
-        nc.vector.quantize_mx(out=codes0[:].bitcast(FP8X4), scales=scales0[:], in_=picked0[:].rearrange("p n j -> p (n j)"))
+            window = cast(0, u)
+            nc.vector.tensor_copy(picked0[:, :, u], window.indirect(offsets[:]))
+        load_scales(0, w1_scales, "pairs01")
+        quantize(slice(0, S), picked0[:])
         for c in range(CHUNKS):
-            cols = slice(c * CHUNK, (c + 1) * CHUNK)
-            multiply(0, c, codes0[:, cols], scales0[:, cols])
+            multiply(0, c)
 
-        picked1 = [keep.tile([P, CHUNK, 4], BF16, name=f"picked1_{c}", align_bytes=64) for c in range(CHUNKS)]
-
-        def gather1(u, c):
+        gathered = keep.tile([P, CHUNKS, 2, CHUNK], U32, name="gathered")
+        window = cast(1, 0)
+        nc.vector.tensor_copy(gathered[:, :, 0, :], window.indirect(offsets[:]))
+        window = cast(1, 1)
+        for c in range(CHUNKS):
             entries = offsets[:, c * LIST_COLS : (c + 1) * LIST_COLS]
-            nc.vector.tensor_copy(words_of(picked1[c])[:, :, u], window(pair_tiles[1, u]).indirect(entries))
-
-        a, b, raw = pieces[1, 0][0]
-        cast(pair_tiles[1, 0], a, b, raw, 352)
+            nc.vector.tensor_copy(gathered[:, c, 1, :], window.indirect(entries))
         for c in range(CHUNKS):
-            gather1(0, c)
-        a, b, raw = pieces[1, 1][0]
-        cast(pair_tiles[1, 1], a, b, raw, b - a)
-        a, b, raw = pieces[1, 1][1]
-        cast(pair_tiles[1, 1], a, b, raw, 160)
+            woven = keep.tile([P, CHUNK, 2], U32, name=f"woven{c}", align_bytes=64)
+            nc.scalar.copy(woven[:], gathered[:, c, :, :].rearrange("p u n -> p n u"))
+            quantize(slice(c * CHUNK, (c + 1) * CHUNK), woven[:])
+            multiply(1, c)
 
-        def quantize1(c):
-            codes = keep.tile([P, CHUNK], U32, name=f"codes1_{c}", align_bytes=64)
-            scales = keep.tile([P, CHUNK], U8, name=f"scales1_{c}", align_bytes=64)
-            nc.vector.quantize_mx(out=codes[:].bitcast(FP8X4), scales=scales[:], in_=picked1[c][:].rearrange("p n j -> p (n j)"))
-            multiply(1, c, codes[:], scales[:])
+        for c in range(CHUNKS):
             width = min(CHUNK, S - 1 - c * CHUNK)
             nc.scalar.copy(tap1[:, 1 + c * CHUNK : 1 + c * CHUNK + width], banks[1, c][:, 0:width])
-
-        def finish(c):
             cols = slice(c * CHUNK, (c + 1) * CHUNK)
             result = keep.tile([M, CHUNK], F32, name=f"result{c}")
             nc.vector.tensor_tensor(result[:], banks[0, c][:], tap1[:, cols], mybir.AluOpType.add)
             nc.sync.dma_start(out[:, cols], result[:])
-
-        gather1(1, 0)
-        for c in range(CHUNKS):
-            if c + 1 < CHUNKS:
-                gather1(1, c + 1)
-            quantize1(c)
-        for c in range(CHUNKS):
-            finish(c)

@@ -20,7 +20,9 @@ CHUNK = 128
 CHUNKS = S // CHUNK
 LIST_COLS = CHUNK // 16
 HALF = T // 2
-VECTOR_COLS = 320
+SLOTS = 4
+SLOT_BYTES = 2 * HALF * 4
+VECTOR_COLS = {(0, 0): 640, (0, 1): 320, (1, 0): 256, (1, 1): 288}
 
 
 def tile_picked_listconv_none_e_kernel(tc, xT, w1_words, w1_scales, w2_words, w2_scales, offs, out):
@@ -29,14 +31,17 @@ def tile_picked_listconv_none_e_kernel(tc, xT, w1_words, w1_scales, w2_words, w2
 
     with ExitStack() as ctx:
         keep = ctx.enter_context(tc.tile_pool(name="keep", bufs=1))
+        staging = ctx.enter_context(tc.tile_pool(name="staging", bufs=1))
         psum = ctx.enter_context(tc.psum_pool(name="psum", bufs=1))
         raw = {}
         w_codes = {}
         w_scales = {}
 
-        def load_x(z, u, h):
-            raw[z, u, h] = keep.tile([P, 2, HALF], F32, name=f"raw{z}{u}{h}", tag="staging", bufs=4, align_bytes=64)
-            nc.sync.dma_start(raw[z, u, h][:], x_rows[z][:, 2 * u : 2 * u + 2, h * HALF : (h + 1) * HALF])
+        def load_x(z, u, start, stop):
+            slot = 2 * u + start // HALF
+            piece = staging.tile([P, 2, stop - start], F32, name=f"raw{z}{u}_{start}", offset=slot * SLOT_BYTES)
+            nc.sync.dma_start(piece[:], x_rows[z][:, 2 * u : 2 * u + 2, start:stop])
+            raw.setdefault((z, u), []).append((start, stop, piece))
 
         def load_scales(d, scales, tag):
             w_scales[d] = keep.tile([P, PASSES, M], U8, name=f"w_scales{d}", tag=tag, align_bytes=64)
@@ -45,54 +50,53 @@ def tile_picked_listconv_none_e_kernel(tc, xT, w1_words, w1_scales, w2_words, w2
             for r in range(4):
                 nc.sync.dma_start(w_scales[d][r:P:32, :, :].bitcast(I32), rows[r].bitcast(I32))
 
-        def load_words(d, words):
-            w_codes[d] = keep.tile([P, PASSES, 2 * M], U8, name=f"w_codes{d}", tag="staging", bufs=4, align_bytes=64)
+        def load_words(d, words, offset):
+            w_codes[d] = staging.tile([P, PASSES, 2 * M], U8, name=f"w_codes{d}", align_bytes=64, offset=offset)
             nc.sync.dma_start(w_codes[d][:].bitcast(I32), words.rearrange("z p c -> p z c").bitcast(I32))
 
-        halves = [(z, u, h) for z in range(PASSES) for u in range(2) for h in range(2)]
-        load_x(*halves[0])
+        load_x(0, 0, 0, T)
         offsets = keep.tile([P, S // 16], U16, name="offsets")
         nc.sync.dma_start(offsets[:], offs)
         load_scales(1, w2_scales, "w_scales1")
-        for half in halves[1:]:
-            load_x(*half)
-        load_words(1, w2_words)
-        load_words(0, w1_words)
+        for z, u in ((0, 1), (1, 0), (1, 1)):
+            load_x(z, u, 0, HALF)
+            load_x(z, u, HALF, T)
+        load_words(1, w2_words, 2048)
+        load_words(0, w1_words, 2048 + 512)
 
         tap1 = keep.tile([P, S], F32, name="tap1")
         nc.gpsimd.memset(tap1[:, 0:1], 0.0)
 
         def cast(z, u):
             pairs = keep.tile([P, T, 2], BF16, name=f"pairs{z}{u}", tag=f"pairs{z}{u}", align_bytes=64)
-            for h in range(2):
-                source = raw[z, u, h][:].rearrange("p e t -> p t e")
-                target = pairs[:, h * HALF : (h + 1) * HALF, :]
-                split = VECTOR_COLS if (h == 1 or (z, u) == (0, 0)) else 0
-                if (z, u, h) == (1, 0, 1):
-                    split = 128
+            for start, stop, piece in raw[z, u]:
+                source = piece[:].rearrange("p e t -> p t e")
+                target = pairs[:, start:stop, :]
+                split = VECTOR_COLS[z, u] if stop == T else 0
                 if split:
                     nc.vector.tensor_copy(target[:, 0:split, :], source[:, 0:split, :])
-                nc.scalar.copy(target[:, split:HALF, :], source[:, split:HALF, :])
+                nc.scalar.copy(target[:, split:, :], source[:, split:, :])
             return pairs[:].rearrange("p t e -> p (t e)").bitcast(U32)
 
         banks = {(d, c): psum.tile([M, CHUNK], F32, name=f"bank{d}{c}") for c in range(CHUNKS) for d in range(2)}
+        codes = [
+            staging.tile([P, S // 2], U32, name=f"codes{i}", align_bytes=64, offset=2 * i * SLOT_BYTES) for i in range(2)
+        ]
+        scales = [keep.tile([P, S // 2], U8, name=f"scales{i}", align_bytes=64) for i in range(2)]
 
-        codes = keep.tile([P, S], U32, name="codes", align_bytes=64)
-        scales = keep.tile([P, S], U8, name="scales", align_bytes=64)
-
-        def quantize(cols, words):
+        def quantize(i, cols, words):
             values = words.rearrange("p n u -> p (n u)").bitcast(BF16)
-            nc.vector.quantize_mx(out=codes[:, cols].bitcast(FP8X4), scales=scales[:, cols], in_=values)
+            nc.vector.quantize_mx(out=codes[i][:, cols].bitcast(FP8X4), scales=scales[i][:, cols], in_=values)
 
         def multiply(z, c):
-            cols = slice(c * CHUNK, (c + 1) * CHUNK)
+            i, cols = c // 2, slice(c % 2 * CHUNK, (c % 2 + 1) * CHUNK)
             for d in (1, 0):
                 nc.tensor.matmul_mx(
                     out=banks[d, c][:],
                     lhsT=w_codes[d][:, z, :].bitcast(FP4X4),
                     lhsT_scale=w_scales[d][:, z, :],
-                    rhs=codes[:, cols].bitcast(FP8X4),
-                    rhs_scale=scales[:, cols],
+                    rhs=codes[i][:, cols].bitcast(FP8X4),
+                    rhs_scale=scales[i][:, cols],
                     start=(z == 0),
                     stop=(z == PASSES - 1),
                 )
@@ -102,21 +106,22 @@ def tile_picked_listconv_none_e_kernel(tc, xT, w1_words, w1_scales, w2_words, w2
             window = cast(0, u)
             nc.vector.tensor_copy(picked0[:, :, u], window.indirect(offsets[:]))
         load_scales(0, w1_scales, "pairs01")
-        quantize(slice(0, S), picked0[:])
-        for c in range(CHUNKS):
-            multiply(0, c)
 
         gathered = keep.tile([P, CHUNKS, 2, CHUNK], U32, name="gathered")
         window = cast(1, 0)
+        quantize(0, slice(0, S // 2), picked0[:, 0 : S // 2, :])
         nc.vector.tensor_copy(gathered[:, :, 0, :], window.indirect(offsets[:]))
         window = cast(1, 1)
+        quantize(1, slice(0, S // 2), picked0[:, S // 2 : S, :])
+        for c in range(CHUNKS):
+            multiply(0, c)
         for c in range(CHUNKS):
             entries = offsets[:, c * LIST_COLS : (c + 1) * LIST_COLS]
             nc.vector.tensor_copy(gathered[:, c, 1, :], window.indirect(entries))
         for c in range(CHUNKS):
             woven = keep.tile([P, CHUNK, 2], U32, name=f"woven{c}", align_bytes=64)
             nc.scalar.copy(woven[:], gathered[:, c, :, :].rearrange("p u n -> p n u"))
-            quantize(slice(c * CHUNK, (c + 1) * CHUNK), woven[:])
+            quantize(c // 2, slice(c % 2 * CHUNK, (c % 2 + 1) * CHUNK), woven[:])
             multiply(1, c)
 
         for c in range(CHUNKS):

@@ -20,7 +20,7 @@ CHUNK = 128
 CHUNKS = S // CHUNK
 LIST_COLS = CHUNK // 16
 HALF = T // 2
-SLOTS = 4
+SLOTS = 5
 SLOT_BYTES = 2 * HALF * 4
 VECTOR_COLS = {(0, 0): 640, (0, 1): 320, (1, 0): 256, (1, 1): 288}
 
@@ -38,7 +38,7 @@ def tile_picked_listconv_none_e_kernel(tc, xT, w1_words, w1_scales, w2_words, w2
         w_scales = {}
 
         def load_x(z, u, start, stop):
-            slot = 2 * u + start // HALF
+            slot = (4 * z + 2 * u + start // HALF) % SLOTS
             piece = staging.tile([P, 2, stop - start], F32, name=f"raw{z}{u}_{start}", offset=slot * SLOT_BYTES)
             nc.sync.dma_start(piece[:], x_rows[z][:, 2 * u : 2 * u + 2, start:stop])
             raw.setdefault((z, u), []).append((start, stop, piece))
@@ -61,8 +61,8 @@ def tile_picked_listconv_none_e_kernel(tc, xT, w1_words, w1_scales, w2_words, w2
         for z, u in ((0, 1), (1, 0), (1, 1)):
             load_x(z, u, 0, HALF)
             load_x(z, u, HALF, T)
-        load_words(1, w2_words, 2048)
-        load_words(0, w1_words, 2048 + 512)
+        load_words(1, w2_words, 4 * SLOT_BYTES + 2048)
+        load_words(0, w1_words, 4 * SLOT_BYTES + 2048 + 512)
 
         tap1 = keep.tile([P, S], F32, name="tap1")
         nc.gpsimd.memset(tap1[:, 0:1], 0.0)
@@ -80,7 +80,7 @@ def tile_picked_listconv_none_e_kernel(tc, xT, w1_words, w1_scales, w2_words, w2
 
         banks = {(d, c): psum.tile([M, CHUNK], F32, name=f"bank{d}{c}") for c in range(CHUNKS) for d in range(2)}
         codes = [
-            staging.tile([P, S // 2], U32, name=f"codes{i}", align_bytes=64, offset=2 * i * SLOT_BYTES) for i in range(2)
+            staging.tile([P, S // 2], U32, name=f"codes{i}", align_bytes=64, offset=(4 + 2 * i) % SLOTS * SLOT_BYTES) for i in range(2)
         ]
         scales = [keep.tile([P, S // 2], U8, name=f"scales{i}", align_bytes=64) for i in range(2)]
 

@@ -22,7 +22,12 @@ LIST_COLS = CHUNK // 16
 HALF = T // 2
 SLOTS = 5
 SLOT_BYTES = 2 * HALF * 4
-VECTOR_COLS = {(0, 0): 640, (0, 1): 320, (1, 0): 256, (1, 1): 288}
+PIECES = {
+    (0, 0): [(0, 1024, 1, 640)],
+    (0, 1): [(0, 512, 9, 0), (512, 1024, 13, 320)],
+    (1, 0): [(0, 512, 17, 0), (512, 1024, 5, 288)],
+    (1, 1): [(0, 512, 1, 0), (512, 1024, 9, 304)],
+}
 
 
 def tile_picked_listconv_none_e_kernel(tc, xT, w1_words, w1_scales, w2_words, w2_scales, offs, out):
@@ -37,15 +42,15 @@ def tile_picked_listconv_none_e_kernel(tc, xT, w1_words, w1_scales, w2_words, w2
         w_codes = {}
         w_scales = {}
 
-        def load_x(z, u, start, stop):
-            slot = (4 * z + 2 * u + start // HALF) % SLOTS
-            piece = staging.tile([P, 2, stop - start], F32, name=f"raw{z}{u}_{start}", offset=slot * SLOT_BYTES)
-            nc.sync.dma_start(piece[:], x_rows[z][:, 2 * u : 2 * u + 2, start:stop])
-            raw.setdefault((z, u), []).append((start, stop, piece))
+        def load_x(z, u):
+            for start, stop, slot, split in PIECES[z, u]:
+                piece = staging.tile([P, 2, stop - start], F32, name=f"raw{z}{u}_{start}", offset=slot * 1024)
+                nc.sync.dma_start(piece[:], x_rows[z][:, 2 * u : 2 * u + 2, start:stop])
+                raw.setdefault((z, u), []).append((start, stop, split, piece))
 
         def load_scales(d, scales, tag):
             w_scales[d] = keep.tile([P, PASSES, M], U8, name=f"w_scales{d}", tag=tag, align_bytes=64)
-            nc.gpsimd.memset(w_scales[d][:].bitcast(I32), 0)
+            (nc.gpsimd if d else nc.vector).memset(w_scales[d][:].bitcast(I32), 0)
             rows = scales.rearrange("z (q r) c -> r q z c", r=4)
             for r in range(4):
                 nc.sync.dma_start(w_scales[d][r:P:32, :, :].bitcast(I32), rows[r].bitcast(I32))
@@ -54,33 +59,32 @@ def tile_picked_listconv_none_e_kernel(tc, xT, w1_words, w1_scales, w2_words, w2
             w_codes[d] = staging.tile([P, PASSES, 2 * M], U8, name=f"w_codes{d}", align_bytes=64, offset=offset)
             nc.sync.dma_start(w_codes[d][:].bitcast(I32), words.rearrange("z p c -> p z c").bitcast(I32))
 
-        load_x(0, 0, 0, T)
+        load_x(0, 0)
         offsets = keep.tile([P, S // 16], U16, name="offsets")
         nc.sync.dma_start(offsets[:], offs)
         load_scales(1, w2_scales, "w_scales1")
         for z, u in ((0, 1), (1, 0), (1, 1)):
-            load_x(z, u, 0, HALF)
-            load_x(z, u, HALF, T)
-        load_words(1, w2_words, 4 * SLOT_BYTES + 2048)
-        load_words(0, w1_words, 4 * SLOT_BYTES + 2048 + 512)
+            load_x(z, u)
+        load_words(1, w2_words, 13 * 1024)
+        load_words(0, w1_words, 13 * 1024 + 512)
 
         tap1 = keep.tile([P, S], F32, name="tap1")
         nc.gpsimd.memset(tap1[:, 0:1], 0.0)
 
         def cast(z, u):
             pairs = keep.tile([P, T, 2], BF16, name=f"pairs{z}{u}", tag=f"pairs{z}{u}", align_bytes=64)
-            for start, stop, piece in raw[z, u]:
+            for start, stop, split, piece in raw[z, u]:
                 source = piece[:].rearrange("p e t -> p t e")
                 target = pairs[:, start:stop, :]
-                split = VECTOR_COLS[z, u] if stop == T else 0
                 if split:
                     nc.vector.tensor_copy(target[:, 0:split, :], source[:, 0:split, :])
-                nc.scalar.copy(target[:, split:, :], source[:, split:, :])
+                if split < stop - start:
+                    nc.scalar.copy(target[:, split:, :], source[:, split:, :])
             return pairs[:].rearrange("p t e -> p (t e)").bitcast(U32)
 
         banks = {(d, c): psum.tile([M, CHUNK], F32, name=f"bank{d}{c}") for c in range(CHUNKS) for d in range(2)}
         codes = [
-            staging.tile([P, S // 2], U32, name=f"codes{i}", align_bytes=64, offset=(4 + 2 * i) % SLOTS * SLOT_BYTES) for i in range(2)
+            staging.tile([P, S // 2], U32, name=f"codes{i}", align_bytes=64, offset=(5 * 1024, 1024)[i]) for i in range(2)
         ]
         scales = [keep.tile([P, S // 2], U8, name=f"scales{i}", align_bytes=64) for i in range(2)]
 
@@ -101,18 +105,21 @@ def tile_picked_listconv_none_e_kernel(tc, xT, w1_words, w1_scales, w2_words, w2
                     stop=(z == PASSES - 1),
                 )
 
-        picked0 = keep.tile([P, S, 2], U32, name="picked0", align_bytes=64)
+        runs0 = keep.tile([P, 2, 2, S // 2], U32, name="runs0")
         for u in range(2):
             window = cast(0, u)
-            nc.vector.tensor_copy(picked0[:, :, u], window.indirect(offsets[:]))
+            nc.vector.tensor_copy(runs0[:, :, u, :], window.indirect(offsets[:]))
         load_scales(0, w1_scales, "pairs01")
 
         gathered = keep.tile([P, CHUNKS, 2, CHUNK], U32, name="gathered")
         window = cast(1, 0)
-        quantize(0, slice(0, S // 2), picked0[:, 0 : S // 2, :])
+        picked0 = [staging.tile([P, S // 2, 2], U32, name=f"picked0{i}", align_bytes=64, offset=(17 + 2 * i) * 1024) for i in range(2)]
+        nc.vector.tensor_copy(picked0[0][:].bitcast(I32), runs0[:, 0, :, :].bitcast(I32).rearrange("p u n -> p n u"))
+        nc.scalar.copy(picked0[1][:], runs0[:, 1, :, :].rearrange("p u n -> p n u"))
         nc.vector.tensor_copy(gathered[:, :, 0, :], window.indirect(offsets[:]))
+        quantize(0, slice(0, S // 2), picked0[0][:])
         window = cast(1, 1)
-        quantize(1, slice(0, S // 2), picked0[:, S // 2 : S, :])
+        quantize(1, slice(0, S // 2), picked0[1][:])
         for c in range(CHUNKS):
             multiply(0, c)
         for c in range(CHUNKS):

@@ -24,9 +24,9 @@ SLOTS = 5
 SLOT_BYTES = 2 * HALF * 4
 PIECES = {
     (0, 0): [(0, 1024, 1, 640)],
-    (0, 1): [(0, 512, 9, 0), (512, 1024, 13, 320)],
-    (1, 0): [(0, 512, 17, 0), (512, 1024, 5, 288)],
-    (1, 1): [(0, 512, 1, 0), (512, 1024, 9, 304)],
+    (0, 1): [(0, 1024, 9, 640)],
+    (1, 0): [(0, 512, 17, 0), (512, 1024, 5, 192)],
+    (1, 1): [(0, 512, 1, 0), (512, 1024, 9, 320)],
 }
 
 
@@ -50,7 +50,7 @@ def tile_picked_listconv_none_e_kernel(tc, xT, w1_words, w1_scales, w2_words, w2
 
         def load_scales(d, scales, tag):
             w_scales[d] = keep.tile([P, PASSES, M], U8, name=f"w_scales{d}", tag=tag, align_bytes=64)
-            (nc.gpsimd if d else nc.vector).memset(w_scales[d][:].bitcast(I32), 0)
+            nc.gpsimd.memset(w_scales[d][:].bitcast(I32), 0)
             rows = scales.rearrange("z (q r) c -> r q z c", r=4)
             for r in range(4):
                 nc.sync.dma_start(w_scales[d][r:P:32, :, :].bitcast(I32), rows[r].bitcast(I32))
@@ -84,7 +84,7 @@ def tile_picked_listconv_none_e_kernel(tc, xT, w1_words, w1_scales, w2_words, w2
 
         banks = {(d, c): psum.tile([M, CHUNK], F32, name=f"bank{d}{c}") for c in range(CHUNKS) for d in range(2)}
         codes = [
-            staging.tile([P, S // 2], U32, name=f"codes{i}", align_bytes=64, offset=(5 * 1024, 1024)[i]) for i in range(2)
+            staging.tile([P, S // 2], U32, name=f"codes{i}", align_bytes=64, offset=(1024, 19 * 1024)[i]) for i in range(2)
         ]
         scales = [keep.tile([P, S // 2], U8, name=f"scales{i}", align_bytes=64) for i in range(2)]
 
@@ -105,21 +105,25 @@ def tile_picked_listconv_none_e_kernel(tc, xT, w1_words, w1_scales, w2_words, w2
                     stop=(z == PASSES - 1),
                 )
 
-        runs0 = keep.tile([P, 2, 2, S // 2], U32, name="runs0")
-        for u in range(2):
-            window = cast(0, u)
-            nc.vector.tensor_copy(runs0[:, :, u, :], window.indirect(offsets[:]))
-        load_scales(0, w1_scales, "pairs01")
+        runs0 = keep.tile([P, 2, S // 2], U32, name="runs0")
+        stepped0 = keep.tile([P, S // 2, 2], U32, name="stepped0", align_bytes=64)
+        first, second = offsets[:, 0 : S // 32], offsets[:, S // 32 : S // 16]
+        window = cast(0, 0)
+        nc.vector.tensor_copy(runs0[:, 0, :], window.indirect(first))
+        nc.vector.tensor_copy(stepped0[:, :, 0], window.indirect(second))
+        window01 = cast(0, 1)
+        nc.vector.tensor_copy(runs0[:, 1, :], window01.indirect(first))
 
         gathered = keep.tile([P, CHUNKS, 2, CHUNK], U32, name="gathered")
         window = cast(1, 0)
-        picked0 = [staging.tile([P, S // 2, 2], U32, name=f"picked0{i}", align_bytes=64, offset=(17 + 2 * i) * 1024) for i in range(2)]
-        nc.vector.tensor_copy(picked0[0][:].bitcast(I32), runs0[:, 0, :, :].bitcast(I32).rearrange("p u n -> p n u"))
-        nc.scalar.copy(picked0[1][:], runs0[:, 1, :, :].rearrange("p u n -> p n u"))
+        nc.vector.tensor_copy(stepped0[:, :, 1], window01.indirect(second))
+        load_scales(0, w1_scales, "pairs01")
+        woven0 = staging.tile([P, S // 2, 2], U32, name="woven0", align_bytes=64, offset=17 * 1024)
+        nc.scalar.copy(woven0[:], runs0[:].rearrange("p u n -> p n u"))
         nc.vector.tensor_copy(gathered[:, :, 0, :], window.indirect(offsets[:]))
-        quantize(0, slice(0, S // 2), picked0[0][:])
+        quantize(1, slice(0, S // 2), stepped0[:])
         window = cast(1, 1)
-        quantize(1, slice(0, S // 2), picked0[1][:])
+        quantize(0, slice(0, S // 2), woven0[:])
         for c in range(CHUNKS):
             multiply(0, c)
         for c in range(CHUNKS):

@@ -13,127 +13,109 @@ U16 = mybir.dt.uint16
 U8 = mybir.dt.uint8
 FP8X4 = mybir.dt.float8_e4m3fn_x4
 FP4X4 = mybir.dt.float4_e2m1fn_x4
+COPY = mybir.ActivationFunctionType.Copy
 
 P = 128
 PASSES = 2
+PACK = 4
 CHUNK = 128
 CHUNKS = S // CHUNK
-LIST_COLS = CHUNK // 16
-HALF = T // 2
-SLOTS = 5
-SLOT_BYTES = 2 * HALF * 4
-PIECES = {
-    (0, 0): [(0, 1024, 1, 640)],
-    (0, 1): [(0, 1024, 9, 640)],
-    (1, 0): [(0, 512, 17, 0), (512, 1024, 5, 192)],
-    (1, 1): [(0, 512, 1, 0), (512, 1024, 9, 320)],
-}
+HALF = S // 2
+SHARE = ((320, 320), (320, 256))
 
 
 def tile_picked_listconv_none_e_kernel(tc, xT, w1_words, w1_scales, w2_words, w2_scales, offs, out):
     nc = tc.nc
-    x_rows = xT.rearrange("(z p j) t -> z p j t", z=PASSES, j=4)
+    x_rows = xT.rearrange("(z p j) t -> z j p t", z=PASSES, j=PACK)
 
     with ExitStack() as ctx:
         keep = ctx.enter_context(tc.tile_pool(name="keep", bufs=1))
-        staging = ctx.enter_context(tc.tile_pool(name="staging", bufs=1))
         psum = ctx.enter_context(tc.psum_pool(name="psum", bufs=1))
-        raw = {}
+        planes = {}
         w_codes = {}
         w_scales = {}
 
-        def load_x(z, u):
-            for start, stop, slot, split in PIECES[z, u]:
-                piece = staging.tile([P, 2, stop - start], F32, name=f"raw{z}{u}_{start}", offset=slot * 1024)
-                nc.sync.dma_start(piece[:], x_rows[z][:, 2 * u : 2 * u + 2, start:stop])
-                raw.setdefault((z, u), []).append((start, stop, split, piece))
+        def load_plane(z, j):
+            planes[z, j] = keep.tile([P, T], F32, name=f"plane{z}{j}")
+            nc.sync.dma_start(planes[z, j][:], x_rows[z, j])
 
-        def load_scales(d, scales, tag):
-            w_scales[d] = keep.tile([P, PASSES, M], U8, name=f"w_scales{d}", tag=tag, align_bytes=64)
-            nc.gpsimd.memset(w_scales[d][:].bitcast(I32), 0)
+        def load_scales(d, scales):
             rows = scales.rearrange("z (q r) c -> r q z c", r=4)
             for r in range(4):
                 nc.sync.dma_start(w_scales[d][r:P:32, :, :].bitcast(I32), rows[r].bitcast(I32))
 
-        def load_words(d, words, offset):
-            w_codes[d] = staging.tile([P, PASSES, 2 * M], U8, name=f"w_codes{d}", align_bytes=64, offset=offset)
+        def load_words(d, words):
+            w_codes[d] = keep.tile([P, PASSES, 2 * M], U8, name=f"w_codes{d}", align_bytes=64)
             nc.sync.dma_start(w_codes[d][:].bitcast(I32), words.rearrange("z p c -> p z c").bitcast(I32))
 
-        load_x(0, 0)
+        for d in (1, 0):
+            w_scales[d] = keep.tile([P, PASSES, M], U8, name=f"w_scales{d}", align_bytes=64)
+            nc.vector.memset(w_scales[d][:].bitcast(I32), 0)
+        tap1 = keep.tile([P, S], F32, name="tap1")
+        zero = keep.tile([P, 1], F32, name="zero")
+        nc.vector.memset(zero[:], 0.0)
+        nc.scalar.copy(tap1[:, 0:1], zero[:])
+
+        load_plane(0, 0)
         offsets = keep.tile([P, S // 16], U16, name="offsets")
         nc.sync.dma_start(offsets[:], offs)
-        load_scales(1, w2_scales, "w_scales1")
-        for z, u in ((0, 1), (1, 0), (1, 1)):
-            load_x(z, u)
-        load_words(1, w2_words, 13 * 1024)
-        load_words(0, w1_words, 13 * 1024 + 512)
+        load_scales(1, w2_scales)
+        for j in range(1, PACK):
+            load_plane(0, j)
+        load_scales(0, w1_scales)
+        load_words(1, w2_words)
+        for j in range(PACK):
+            load_plane(1, j)
+        load_words(0, w1_words)
 
-        tap1 = keep.tile([P, S], F32, name="tap1")
-        nc.gpsimd.memset(tap1[:, 0:1], 0.0)
-
-        def cast(z, u):
-            pairs = keep.tile([P, T, 2], BF16, name=f"pairs{z}{u}", tag=f"pairs{z}{u}", align_bytes=64)
-            for start, stop, split, piece in raw[z, u]:
-                source = piece[:].rearrange("p e t -> p t e")
-                target = pairs[:, start:stop, :]
-                if split:
-                    nc.vector.tensor_copy(target[:, 0:split, :], source[:, 0:split, :])
-                if split < stop - start:
-                    nc.scalar.copy(target[:, split:, :], source[:, split:, :])
-            return pairs[:].rearrange("p t e -> p (t e)").bitcast(U32)
+        def entries(first, count):
+            return offsets[:, first // 16 : (first + count) // 16]
 
         banks = {(d, c): psum.tile([M, CHUNK], F32, name=f"bank{d}{c}") for c in range(CHUNKS) for d in range(2)}
-        codes = [
-            staging.tile([P, S // 2], U32, name=f"codes{i}", align_bytes=64, offset=(1024, 19 * 1024)[i]) for i in range(2)
-        ]
-        scales = [keep.tile([P, S // 2], U8, name=f"scales{i}", align_bytes=64) for i in range(2)]
 
-        def quantize(i, cols, words):
-            values = words.rearrange("p n u -> p (n u)").bitcast(BF16)
-            nc.vector.quantize_mx(out=codes[i][:, cols].bitcast(FP8X4), scales=scales[i][:, cols], in_=values)
-
-        def multiply(z, c):
-            i, cols = c // 2, slice(c % 2 * CHUNK, (c % 2 + 1) * CHUNK)
+        def multiply(z, c, codes, scales):
             for d in (1, 0):
                 nc.tensor.matmul_mx(
                     out=banks[d, c][:],
                     lhsT=w_codes[d][:, z, :].bitcast(FP4X4),
                     lhsT_scale=w_scales[d][:, z, :],
-                    rhs=codes[i][:, cols].bitcast(FP8X4),
-                    rhs_scale=scales[i][:, cols],
+                    rhs=codes.bitcast(FP8X4),
+                    rhs_scale=scales,
                     start=(z == 0),
                     stop=(z == PASSES - 1),
                 )
 
-        runs0 = keep.tile([P, 2, S // 2], U32, name="runs0")
-        stepped0 = keep.tile([P, S // 2, 2], U32, name="stepped0", align_bytes=64)
-        first, second = offsets[:, 0 : S // 32], offsets[:, S // 32 : S // 16]
-        window = cast(0, 0)
-        nc.vector.tensor_copy(runs0[:, 0, :], window.indirect(first))
-        nc.vector.tensor_copy(stepped0[:, :, 0], window.indirect(second))
-        window01 = cast(0, 1)
-        nc.vector.tensor_copy(runs0[:, 1, :], window01.indirect(first))
-
-        gathered = keep.tile([P, CHUNKS, 2, CHUNK], U32, name="gathered")
-        window = cast(1, 0)
-        nc.vector.tensor_copy(stepped0[:, :, 1], window01.indirect(second))
-        load_scales(0, w1_scales, "pairs01")
-        woven0 = staging.tile([P, S // 2, 2], U32, name="woven0", align_bytes=64, offset=17 * 1024)
-        nc.scalar.copy(woven0[:], runs0[:].rearrange("p u n -> p n u"))
-        nc.vector.tensor_copy(gathered[:, :, 0, :], window.indirect(offsets[:]))
-        quantize(1, slice(0, S // 2), stepped0[:])
-        window = cast(1, 1)
-        quantize(0, slice(0, S // 2), woven0[:])
-        for c in range(CHUNKS):
-            multiply(0, c)
-        for c in range(CHUNKS):
-            entries = offsets[:, c * LIST_COLS : (c + 1) * LIST_COLS]
-            nc.vector.tensor_copy(gathered[:, c, 1, :], window.indirect(entries))
-        for c in range(CHUNKS):
-            woven = keep.tile([P, CHUNK, 2], U32, name=f"woven{c}", align_bytes=64)
-            nc.scalar.copy(woven[:], gathered[:, c, :, :].rearrange("p u n -> p n u"))
-            quantize(c // 2, slice(c % 2 * CHUNK, (c % 2 + 1) * CHUNK), woven[:])
-            multiply(1, c)
+        for z in range(PASSES):
+            last = z == PASSES - 1
+            woven = keep.tile([P, S, PACK], BF16, name=f"woven{z}", align_bytes=64)
+            for j in range(PACK):
+                window = planes[z, j][:]
+                u, e = divmod(j, 2)
+                share = SHARE[z][u]
+                pieces = 2 if last and j == PACK - 1 else 1
+                for i in range(pieces):
+                    n = share // pieces
+                    nc.vector.tensor_copy(woven[:, i * n : (i + 1) * n, j], window.indirect(entries(i * n, n)))
+                n = (S - share) // pieces
+                if e == 0:
+                    runs = keep.tile([P, 2, S - share], BF16, name=f"runs{z}{u}")
+                for i in range(pieces):
+                    nc.scalar.activation(runs[:, e, i * n : (i + 1) * n], window.indirect(entries(share + i * n, n)), COPY)
+                if e == 1:
+                    for i in range(pieces):
+                        nc.scalar.copy(
+                            woven[:, share + i * n : share + (i + 1) * n, 2 * u : 2 * u + 2],
+                            runs[:, :, i * n : (i + 1) * n].rearrange("p e n -> p n e"),
+                        )
+            width = CHUNK if last else HALF
+            for first in range(0, S, width):
+                codes = keep.tile([P, width], U32, name=f"codes{z}_{first}", align_bytes=64)
+                scales = keep.tile([P, width], U8, name=f"scales{z}_{first}", align_bytes=64)
+                values = woven[:, first : first + width, :].rearrange("p n j -> p (n j)")
+                nc.vector.quantize_mx(out=codes[:].bitcast(FP8X4), scales=scales[:], in_=values)
+                for i in range(width // CHUNK):
+                    cols = slice(i * CHUNK, (i + 1) * CHUNK)
+                    multiply(z, first // CHUNK + i, codes[:, cols], scales[:, cols])
 
         for c in range(CHUNKS):
             width = min(CHUNK, S - 1 - c * CHUNK)

@@ -21,7 +21,10 @@ PACK = 4
 CHUNK = 128
 CHUNKS = S // CHUNK
 HALF = S // 2
-SHARE = ((320, 320), (320, 256))
+SHARED = 2
+SHARE = ((288, 288), (288, 256))
+SLOTS = 5
+SLOT_BYTES = T * 4
 
 
 def tile_picked_listconv_none_e_kernel(tc, xT, w1_words, w1_scales, w2_words, w2_scales, offs, out):
@@ -30,66 +33,70 @@ def tile_picked_listconv_none_e_kernel(tc, xT, w1_words, w1_scales, w2_words, w2
 
     with ExitStack() as ctx:
         keep = ctx.enter_context(tc.tile_pool(name="keep", bufs=1))
+        staging = ctx.enter_context(tc.tile_pool(name="staging", bufs=1))
         psum = ctx.enter_context(tc.psum_pool(name="psum", bufs=1))
         planes = {}
         w_codes = {}
         w_scales = {}
 
-        def load_plane(z, j):
-            planes[z, j] = keep.tile([P, T], F32, name=f"plane{z}{j}")
-            nc.sync.dma_start(planes[z, j][:], x_rows[z, j])
+        def load_plane(i):
+            planes[i] = staging.tile([P, T], F32, name=f"plane{i}", offset=i % SLOTS * SLOT_BYTES)
+            nc.sync.dma_start(planes[i][:], x_rows[i // PACK, i % PACK])
 
-        def load_scales(d, scales):
+        def load_scales(d, scales, offset):
+            w_scales[d] = staging.tile([P, PASSES, M], U8, name=f"w_scales{d}", align_bytes=64, offset=offset)
+            nc.vector.memset(w_scales[d][:].bitcast(I32), 0)
             rows = scales.rearrange("z (q r) c -> r q z c", r=4)
             for r in range(4):
                 nc.sync.dma_start(w_scales[d][r:P:32, :, :].bitcast(I32), rows[r].bitcast(I32))
 
-        def load_words(d, words):
-            w_codes[d] = keep.tile([P, PASSES, 2 * M], U8, name=f"w_codes{d}", align_bytes=64)
+        def load_words(d, words, offset):
+            w_codes[d] = staging.tile([P, PASSES, 2 * M], U8, name=f"w_codes{d}", align_bytes=64, offset=offset)
             nc.sync.dma_start(w_codes[d][:].bitcast(I32), words.rearrange("z p c -> p z c").bitcast(I32))
 
-        for d in (1, 0):
-            w_scales[d] = keep.tile([P, PASSES, M], U8, name=f"w_scales{d}", align_bytes=64)
-            nc.vector.memset(w_scales[d][:].bitcast(I32), 0)
         tap1 = keep.tile([P, S], F32, name="tap1")
         zero = keep.tile([P, 1], F32, name="zero")
         nc.vector.memset(zero[:], 0.0)
         nc.scalar.copy(tap1[:, 0:1], zero[:])
 
-        load_plane(0, 0)
+        load_plane(0)
         offsets = keep.tile([P, S // 16], U16, name="offsets")
         nc.sync.dma_start(offsets[:], offs)
-        load_scales(1, w2_scales)
-        for j in range(1, PACK):
-            load_plane(0, j)
-        load_scales(0, w1_scales)
-        load_words(1, w2_words)
-        for j in range(PACK):
-            load_plane(1, j)
-        load_words(0, w1_words)
+        for i in range(1, SLOTS):
+            load_plane(i)
+        spare = SLOTS * SLOT_BYTES
+        load_scales(1, w2_scales, spare + 1024)
 
         def entries(first, count):
             return offsets[:, first // 16 : (first + count) // 16]
 
-        banks = {(d, c): psum.tile([M, CHUNK], F32, name=f"bank{d}{c}") for c in range(CHUNKS) for d in range(2)}
+        banks = {}
+        for c in range(CHUNKS):
+            if c < SHARED:
+                both = psum.tile([M, 2, CHUNK], F32, name=f"bank{c}")
+                banks[0, c], banks[1, c] = both[:, 0, :], both[:, 1, :]
+            else:
+                for d in range(2):
+                    banks[d, c] = psum.tile([M, CHUNK], F32, name=f"bank{d}{c}")[:]
 
         def multiply(z, c, codes, scales):
             for d in (1, 0):
                 nc.tensor.matmul_mx(
-                    out=banks[d, c][:],
+                    out=banks[d, c],
                     lhsT=w_codes[d][:, z, :].bitcast(FP4X4),
                     lhsT_scale=w_scales[d][:, z, :],
                     rhs=codes.bitcast(FP8X4),
                     rhs_scale=scales,
-                    start=(z == 0),
-                    stop=(z == PASSES - 1),
+                    start=(z == 0 and (d == 1 or c >= SHARED)),
+                    stop=(z == PASSES - 1 and (d == 0 or c >= SHARED)),
                 )
 
         for z in range(PASSES):
             last = z == PASSES - 1
             woven = keep.tile([P, S, PACK], BF16, name=f"woven{z}", align_bytes=64)
             for j in range(PACK):
-                window = planes[z, j][:]
+                plane = z * PACK + j
+                window = planes[plane][:]
                 u, e = divmod(j, 2)
                 share = SHARE[z][u]
                 pieces = 2 if last and j == PACK - 1 else 1
@@ -97,7 +104,9 @@ def tile_picked_listconv_none_e_kernel(tc, xT, w1_words, w1_scales, w2_words, w2
                     n = share // pieces
                     nc.vector.tensor_copy(woven[:, i * n : (i + 1) * n, j], window.indirect(entries(i * n, n)))
                 n = (S - share) // pieces
-                if e == 0:
+                if plane == 0:
+                    runs = staging.tile([P, 2, S - share], BF16, name="runs00", offset=spare)
+                elif e == 0:
                     runs = keep.tile([P, 2, S - share], BF16, name=f"runs{z}{u}")
                 for i in range(pieces):
                     nc.scalar.activation(runs[:, e, i * n : (i + 1) * n], window.indirect(entries(share + i * n, n)), COPY)
@@ -107,12 +116,25 @@ def tile_picked_listconv_none_e_kernel(tc, xT, w1_words, w1_scales, w2_words, w2
                             woven[:, share + i * n : share + (i + 1) * n, 2 * u : 2 * u + 2],
                             runs[:, :, i * n : (i + 1) * n].rearrange("p e n -> p n e"),
                         )
+                if plane + SLOTS < PASSES * PACK:
+                    load_plane(plane + SLOTS)
+                if plane == 1:
+                    load_words(1, w2_words, spare)
+                if plane == 3:
+                    load_words(0, w1_words, 3 * SLOT_BYTES)
+                    load_scales(0, w1_scales, 3 * SLOT_BYTES + 512)
             width = CHUNK if last else HALF
             for first in range(0, S, width):
-                codes = keep.tile([P, width], U32, name=f"codes{z}_{first}", align_bytes=64)
-                scales = keep.tile([P, width], U8, name=f"scales{z}_{first}", align_bytes=64)
+                if last and first >= HALF:
+                    codes = late_codes[:, first - HALF : first - HALF + width]
+                    scales = late_scales[:, 2 * CHUNK - width - (first - HALF) : 2 * CHUNK - (first - HALF)]
+                else:
+                    codes = keep.tile([P, width], U32, name=f"codes{z}_{first}", align_bytes=64)[:]
+                    scales = keep.tile([P, width], U8, name=f"scales{z}_{first}", align_bytes=64)[:]
+                    if z == 0:
+                        late_codes, late_scales = codes, scales
                 values = woven[:, first : first + width, :].rearrange("p n j -> p (n j)")
-                nc.vector.quantize_mx(out=codes[:].bitcast(FP8X4), scales=scales[:], in_=values)
+                nc.vector.quantize_mx(out=codes.bitcast(FP8X4), scales=scales, in_=values)
                 for i in range(width // CHUNK):
                     cols = slice(i * CHUNK, (i + 1) * CHUNK)
                     multiply(z, first // CHUNK + i, codes[:, cols], scales[:, cols])
@@ -122,5 +144,5 @@ def tile_picked_listconv_none_e_kernel(tc, xT, w1_words, w1_scales, w2_words, w2
             nc.scalar.copy(tap1[:, 1 + c * CHUNK : 1 + c * CHUNK + width], banks[1, c][:, 0:width])
             cols = slice(c * CHUNK, (c + 1) * CHUNK)
             result = keep.tile([M, CHUNK], F32, name=f"result{c}")
-            nc.vector.tensor_tensor(result[:], banks[0, c][:], tap1[:, cols], mybir.AluOpType.add)
+            nc.vector.tensor_tensor(result[:], banks[0, c], tap1[:, cols], mybir.AluOpType.add)
             nc.sync.dma_start(out[:, cols], result[:])

@@ -43,12 +43,12 @@ def tile_picked_listconv_none_e_kernel(tc, xT, w1_words, w1_scales, w2_words, w2
             planes[i] = staging.tile([P, T], F32, name=f"plane{i}", offset=i % SLOTS * SLOT_BYTES)
             nc.sync.dma_start(planes[i][:], x_rows[i // PACK, i % PACK])
 
-        def load_scales(d, scales, offset):
+        def load_scales(d, scales, offset, queue):
             w_scales[d] = staging.tile([P, PASSES, M], U8, name=f"w_scales{d}", align_bytes=64, offset=offset)
             nc.vector.memset(w_scales[d][:].bitcast(I32), 0)
             rows = scales.rearrange("z (q r) c -> r q z c", r=4)
             for r in range(4):
-                nc.sync.dma_start(w_scales[d][r:P:32, :, :].bitcast(I32), rows[r].bitcast(I32))
+                queue.dma_start(w_scales[d][r:P:32, :, :].bitcast(I32), rows[r].bitcast(I32))
 
         def load_words(d, words, offset):
             w_codes[d] = staging.tile([P, PASSES, 2 * M], U8, name=f"w_codes{d}", align_bytes=64, offset=offset)
@@ -65,7 +65,7 @@ def tile_picked_listconv_none_e_kernel(tc, xT, w1_words, w1_scales, w2_words, w2
         for i in range(1, SLOTS):
             load_plane(i)
         spare = SLOTS * SLOT_BYTES
-        load_scales(1, w2_scales, spare + 1024)
+        load_scales(1, w2_scales, spare + 1024, nc.scalar)
 
         def entries(first, count):
             return offsets[:, first // 16 : (first + count) // 16]
@@ -122,7 +122,7 @@ def tile_picked_listconv_none_e_kernel(tc, xT, w1_words, w1_scales, w2_words, w2
                     load_words(1, w2_words, spare)
                 if plane == 3:
                     load_words(0, w1_words, 3 * SLOT_BYTES)
-                    load_scales(0, w1_scales, 3 * SLOT_BYTES + 512)
+                    load_scales(0, w1_scales, 3 * SLOT_BYTES + 512, nc.sync)
             width = CHUNK if last else HALF
             for first in range(0, S, width):
                 if last and first >= HALF:

@@ -50,9 +50,11 @@ def tile_picked_listconv_none_e_kernel(tc, xT, w1_words, w1_scales, w2_words, w2
             for r in range(4):
                 queue.dma_start(w_scales[d][r:P:32, :, :].bitcast(I32), rows[r].bitcast(I32))
 
-        def load_words(d, words, offset):
-            w_codes[d] = staging.tile([P, PASSES, 2 * M], U8, name=f"w_codes{d}", align_bytes=64, offset=offset)
-            nc.sync.dma_start(w_codes[d][:].bitcast(I32), words.rearrange("z p c -> p z c").bitcast(I32))
+        def load_words(d, words, first, end, offset):
+            tile = staging.tile([P, end - first, 2 * M], U8, name=f"w_codes{d}{first}", align_bytes=64, offset=offset)
+            nc.sync.dma_start(tile[:].bitcast(I32), words[first:end].rearrange("z p c -> p z c").bitcast(I32))
+            for z in range(first, end):
+                w_codes[d, z] = tile[:, z - first, :]
 
         tap1 = keep.tile([P, S], F32, name="tap1")
         zero = keep.tile([P, 1], F32, name="zero")
@@ -83,7 +85,7 @@ def tile_picked_listconv_none_e_kernel(tc, xT, w1_words, w1_scales, w2_words, w2
             for d in (1, 0):
                 nc.tensor.matmul_mx(
                     out=banks[d, c],
-                    lhsT=w_codes[d][:, z, :].bitcast(FP4X4),
+                    lhsT=w_codes[d, z].bitcast(FP4X4),
                     lhsT_scale=w_scales[d][:, z, :],
                     rhs=codes.bitcast(FP8X4),
                     rhs_scale=scales,
@@ -119,10 +121,12 @@ def tile_picked_listconv_none_e_kernel(tc, xT, w1_words, w1_scales, w2_words, w2
                 if plane + SLOTS < PASSES * PACK:
                     load_plane(plane + SLOTS)
                 if plane == 1:
-                    load_words(1, w2_words, spare)
+                    load_words(1, w2_words, 0, 1, spare)
                 if plane == 3:
-                    load_words(0, w1_words, 3 * SLOT_BYTES)
+                    load_words(0, w1_words, 0, 2, 3 * SLOT_BYTES)
                     load_scales(0, w1_scales, 3 * SLOT_BYTES + 512, nc.sync)
+                if plane == 4:
+                    load_words(1, w2_words, 1, 2, 4 * SLOT_BYTES)
             width = CHUNK if last else HALF
             for first in range(0, S, width):
                 if last and first >= HALF:

@@ -66,8 +66,7 @@ def tile_picked_listconv_none_e_kernel(tc, xT, w1_words, w1_scales, w2_words, w2
         nc.sync.dma_start(offsets[:], offs)
         for i in range(1, SLOTS):
             load_plane(i)
-        spare = SLOTS * SLOT_BYTES
-        load_scales(1, w2_scales, spare + 1024, nc.scalar)
+        load_scales(1, w2_scales, SLOTS * SLOT_BYTES, nc.scalar)
 
         def entries(first, count):
             return offsets[:, first // 16 : (first + count) // 16]
@@ -106,9 +105,7 @@ def tile_picked_listconv_none_e_kernel(tc, xT, w1_words, w1_scales, w2_words, w2
                     n = share // pieces
                     nc.vector.tensor_copy(woven[:, i * n : (i + 1) * n, j], window.indirect(entries(i * n, n)))
                 n = (S - share) // pieces
-                if plane == 0:
-                    runs = staging.tile([P, 2, S - share], BF16, name="runs00", offset=spare)
-                elif e == 0:
+                if e == 0:
                     runs = keep.tile([P, 2, S - share], BF16, name=f"runs{z}{u}")
                 for i in range(pieces):
                     nc.scalar.activation(runs[:, e, i * n : (i + 1) * n], window.indirect(entries(share + i * n, n)), COPY)
@@ -120,9 +117,8 @@ def tile_picked_listconv_none_e_kernel(tc, xT, w1_words, w1_scales, w2_words, w2
                         )
                 if plane + SLOTS < PASSES * PACK:
                     load_plane(plane + SLOTS)
-                if plane == 1:
-                    load_words(1, w2_words, 0, 1, spare)
                 if plane == 3:
+                    load_words(1, w2_words, 0, 1, 3 * SLOT_BYTES + 1024)
                     load_words(0, w1_words, 0, 2, 3 * SLOT_BYTES)
                     load_scales(0, w1_scales, 3 * SLOT_BYTES + 512, nc.sync)
                 if plane == 4:

@@ -21,7 +21,7 @@ PACK = 4
 CHUNK = 128
 CHUNKS = S // CHUNK
 HALF = S // 2
-SHARED = 2
+SHARED = 1
 SHARE = ((288, 288), (288, 256))
 SLOTS = 5
 SLOT_BYTES = T * 4
@@ -80,17 +80,16 @@ def tile_picked_listconv_none_e_kernel(tc, xT, w1_words, w1_scales, w2_words, w2
                 for d in range(2):
                     banks[d, c] = psum.tile([M, CHUNK], F32, name=f"bank{d}{c}")[:]
 
-        def multiply(z, c, codes, scales):
-            for d in (1, 0):
-                nc.tensor.matmul_mx(
-                    out=banks[d, c],
-                    lhsT=w_codes[d, z].bitcast(FP4X4),
-                    lhsT_scale=w_scales[d][:, z, :],
-                    rhs=codes.bitcast(FP8X4),
-                    rhs_scale=scales,
-                    start=(z == 0 and (d == 1 or c >= SHARED)),
-                    stop=(z == PASSES - 1 and (d == 0 or c >= SHARED)),
-                )
+        def multiply(z, d, c, codes, scales):
+            nc.tensor.matmul_mx(
+                out=banks[d, c],
+                lhsT=w_codes[d, z].bitcast(FP4X4),
+                lhsT_scale=w_scales[d][:, z, :],
+                rhs=codes.bitcast(FP8X4),
+                rhs_scale=scales,
+                start=(z == 0 and (d == 1 or c >= SHARED)),
+                stop=(z == PASSES - 1 and (d == 0 or c >= SHARED)),
+            )
 
         for z in range(PASSES):
             last = z == PASSES - 1
@@ -120,24 +119,30 @@ def tile_picked_listconv_none_e_kernel(tc, xT, w1_words, w1_scales, w2_words, w2
                 if plane == 3:
                     load_words(1, w2_words, 0, 1, 3 * SLOT_BYTES + 1024)
                     load_words(0, w1_words, 0, 2, 3 * SLOT_BYTES)
+                    load_words(1, w2_words, 1, 2, 3 * SLOT_BYTES + 1280)
                     load_scales(0, w1_scales, 3 * SLOT_BYTES + 512, nc.sync)
-                if plane == 4:
-                    load_words(1, w2_words, 1, 2, 4 * SLOT_BYTES)
             width = CHUNK if last else HALF
+            quantised = {}
             for first in range(0, S, width):
-                if last and first >= HALF:
-                    codes = late_codes[:, first - HALF : first - HALF + width]
-                    scales = late_scales[:, 2 * CHUNK - width - (first - HALF) : 2 * CHUNK - (first - HALF)]
+                c = first // CHUNK
+                codes = keep.tile([P, width], U32, name=f"codes{z}_{first}", align_bytes=64)[:]
+                if last and c >= 1:
+                    scales = first_codes.bitcast(U8)[:, (c - 1) * CHUNK : c * CHUNK]
                 else:
-                    codes = keep.tile([P, width], U32, name=f"codes{z}_{first}", align_bytes=64)[:]
                     scales = keep.tile([P, width], U8, name=f"scales{z}_{first}", align_bytes=64)[:]
-                    if z == 0:
-                        late_codes, late_scales = codes, scales
+                if z == 0 and c == 0:
+                    first_codes = codes
                 values = woven[:, first : first + width, :].rearrange("p n j -> p (n j)")
                 nc.vector.quantize_mx(out=codes.bitcast(FP8X4), scales=scales, in_=values)
                 for i in range(width // CHUNK):
                     cols = slice(i * CHUNK, (i + 1) * CHUNK)
-                    multiply(z, first // CHUNK + i, codes[:, cols], scales[:, cols])
+                    quantised[first // CHUNK + i] = codes[:, cols], scales[:, cols]
+            if last:
+                order = [(d, c) for c in range(CHUNKS) for d in (1, 0)]
+            else:
+                order = [(d, c) for d in (1, 0) for c in range(CHUNKS)]
+            for d, c in order:
+                multiply(z, d, c, *quantised[c])
 
         for c in range(CHUNKS):
             width = min(CHUNK, S - 1 - c * CHUNK)

from contextlib import ExitStack

import concourse.mybir as mybir

K, T, S, M = 1024, 1024, 512, 128
FLOPS = 2 * 2 * K * M * S

F32 = mybir.dt.float32
BF16 = mybir.dt.bfloat16
I32 = mybir.dt.int32
U32 = mybir.dt.uint32
U16 = mybir.dt.uint16
U8 = mybir.dt.uint8
FP8X4 = mybir.dt.float8_e4m3fn_x4
FP4X4 = mybir.dt.float4_e2m1fn_x4
COPY = mybir.ActivationFunctionType.Copy

P = 128
PASSES = 2
PACK = 4
CHUNK = 128
CHUNKS = S // CHUNK
HALF = S // 2
SHARED = 1
SHARE = ((288, 288), (288, 256))
SLOTS = 5
SLOT_BYTES = T * 4


def tile_picked_listconv_none_e_kernel(tc, xT, w1_words, w1_scales, w2_words, w2_scales, offs, out):
    nc = tc.nc
    x_rows = xT.rearrange("(z p j) t -> z j p t", z=PASSES, j=PACK)

    with ExitStack() as ctx:
        keep = ctx.enter_context(tc.tile_pool(name="keep", bufs=1))
        staging = ctx.enter_context(tc.tile_pool(name="staging", bufs=1))
        psum = ctx.enter_context(tc.psum_pool(name="psum", bufs=1))
        planes = {}
        w_codes = {}
        w_scales = {}

        def load_plane(i):
            planes[i] = staging.tile([P, T], F32, name=f"plane{i}", offset=i % SLOTS * SLOT_BYTES)
            nc.sync.dma_start(planes[i][:], x_rows[i // PACK, i % PACK])

        def load_scales(d, scales, offset, queue):
            w_scales[d] = staging.tile([P, PASSES, M], U8, name=f"w_scales{d}", align_bytes=64, offset=offset)
            nc.vector.memset(w_scales[d][:].bitcast(I32), 0)
            rows = scales.rearrange("z (q r) c -> r q z c", r=4)
            for r in range(4):
                queue.dma_start(w_scales[d][r:P:32, :, :].bitcast(I32), rows[r].bitcast(I32))

        def load_words(d, words, first, end, offset):
            tile = staging.tile([P, end - first, 2 * M], U8, name=f"w_codes{d}{first}", align_bytes=64, offset=offset)
            nc.sync.dma_start(tile[:].bitcast(I32), words[first:end].rearrange("z p c -> p z c").bitcast(I32))
            for z in range(first, end):
                w_codes[d, z] = tile[:, z - first, :]

        tap1 = keep.tile([P, S], F32, name="tap1")
        zero = keep.tile([P, 1], F32, name="zero")
        nc.vector.memset(zero[:], 0.0)
        nc.scalar.copy(tap1[:, 0:1], zero[:])

        load_plane(0)
        offsets = keep.tile([P, S // 16], U16, name="offsets")
        nc.sync.dma_start(offsets[:], offs)
        for i in range(1, SLOTS):
            load_plane(i)
        load_scales(1, w2_scales, SLOTS * SLOT_BYTES, nc.scalar)

        def entries(first, count):
            return offsets[:, first // 16 : (first + count) // 16]

        banks = {}
        for c in range(CHUNKS):
            if c < SHARED:
                both = psum.tile([M, 2, CHUNK], F32, name=f"bank{c}")
                banks[0, c], banks[1, c] = both[:, 0, :], both[:, 1, :]
            else:
                for d in range(2):
                    banks[d, c] = psum.tile([M, CHUNK], F32, name=f"bank{d}{c}")[:]

        def multiply(z, d, c, codes, scales):
            nc.tensor.matmul_mx(
                out=banks[d, c],
                lhsT=w_codes[d, z].bitcast(FP4X4),
                lhsT_scale=w_scales[d][:, z, :],
                rhs=codes.bitcast(FP8X4),
                rhs_scale=scales,
                start=(z == 0 and (d == 1 or c >= SHARED)),
                stop=(z == PASSES - 1 and (d == 0 or c >= SHARED)),
            )

        for z in range(PASSES):
            last = z == PASSES - 1
            woven = keep.tile([P, S, PACK], BF16, name=f"woven{z}", align_bytes=64)
            for j in range(PACK):
                plane = z * PACK + j
                window = planes[plane][:]
                u, e = divmod(j, 2)
                share = SHARE[z][u]
                pieces = 2 if last and j == PACK - 1 else 1
                for i in range(pieces):
                    n = share // pieces
                    nc.vector.tensor_copy(woven[:, i * n : (i + 1) * n, j], window.indirect(entries(i * n, n)))
                n = (S - share) // pieces
                if e == 0:
                    runs = keep.tile([P, 2, S - share], BF16, name=f"runs{z}{u}")
                for i in range(pieces):
                    nc.scalar.activation(runs[:, e, i * n : (i + 1) * n], window.indirect(entries(share + i * n, n)), COPY)
                if e == 1:
                    for i in range(pieces):
                        nc.scalar.copy(
                            woven[:, share + i * n : share + (i + 1) * n, 2 * u : 2 * u + 2],
                            runs[:, :, i * n : (i + 1) * n].rearrange("p e n -> p n e"),
                        )
                if plane + SLOTS < PASSES * PACK:
                    load_plane(plane + SLOTS)
                if plane == 3:
                    load_words(1, w2_words, 0, 1, 3 * SLOT_BYTES + 1024)
                    load_words(0, w1_words, 0, 2, 3 * SLOT_BYTES)
                    load_words(1, w2_words, 1, 2, 3 * SLOT_BYTES + 1280)
                    load_scales(0, w1_scales, 3 * SLOT_BYTES + 512, nc.sync)
            width = CHUNK if last else HALF
            quantised = {}
            for first in range(0, S, width):
                c = first // CHUNK
                codes = keep.tile([P, width], U32, name=f"codes{z}_{first}", align_bytes=64)[:]
                if last and c >= 1:
                    scales = first_codes.bitcast(U8)[:, (c - 1) * CHUNK : c * CHUNK]
                else:
                    scales = keep.tile([P, width], U8, name=f"scales{z}_{first}", align_bytes=64)[:]
                if z == 0 and c == 0:
                    first_codes = codes
                values = woven[:, first : first + width, :].rearrange("p n j -> p (n j)")
                nc.vector.quantize_mx(out=codes.bitcast(FP8X4), scales=scales, in_=values)
                for i in range(width // CHUNK):
                    cols = slice(i * CHUNK, (i + 1) * CHUNK)
                    quantised[first // CHUNK + i] = codes[:, cols], scales[:, cols]
            if last:
                order = [(d, c) for c in range(CHUNKS) for d in (1, 0)]
            else:
                order = [(d, c) for d in (1, 0) for c in range(CHUNKS)]
            for d, c in order:
                multiply(z, d, c, *quantised[c])

        for c in range(CHUNKS):
            width = min(CHUNK, S - 1 - c * CHUNK)
            nc.scalar.copy(tap1[:, 1 + c * CHUNK : 1 + c * CHUNK + width], banks[1, c][:, 0:width])
            cols = slice(c * CHUNK, (c + 1) * CHUNK)
            result = keep.tile([M, CHUNK], F32, name=f"result{c}")
            nc.vector.tensor_tensor(result[:], banks[0, c], tap1[:, cols], mybir.AluOpType.add)
            nc.sync.dma_start(out[:, cols], result[:])
